import numpy as np
import ml_dtypes


def mxq(x, axis, fmt="e4m3"):
    dtype, down = {"e4m3": (ml_dtypes.float8_e4m3fn, 7), "e5m2": (ml_dtypes.float8_e5m2, 14)}[fmt]
    v = np.moveaxis(np.asarray(x, np.float32).astype(ml_dtypes.bfloat16).astype(np.float64), axis, -1)
    blocks = v.reshape(v.shape[:-1] + (-1, 32))
    amax = np.abs(blocks).max(-1, keepdims=True)
    byte = np.maximum(np.where(amax > 0, np.frexp(amax)[1] - 1 + 127, 0) - down, 1)
    scale = np.exp2(byte - 127.0)
    codes = (blocks / scale).astype(np.float32).astype(dtype).astype(np.float64)
    return np.moveaxis((codes * scale).reshape(v.shape), -1, axis)


WIDE = False


def mx_kscale(k):
    if not WIDE:
        return np.ones(k)
    levels = np.array([10, -10, 5, -5, 0])
    if k % 512:
        return np.exp2(np.random.permutation(np.resize(levels, k // 32))).repeat(32)
    a = np.empty((k // 512, 16))
    for p in range(k // 512):
        a[p, :8] = np.random.permutation(np.resize(levels, 8))
        for g in range(8):
            far = levels[np.abs(levels - a[p, g]) >= 10]
            a[p, g + 8] = far[np.random.randint(len(far))]
    return np.exp2(a.ravel()).repeat(32)


def f64(x):
    return np.asarray(x).astype(np.float64)


def striped(idx):
    return np.tile(idx.reshape(-1, 16).T, (8, 1)).astype(np.uint16)


def unstriped(offs):
    return offs[:16].T.reshape(-1).astype(np.int64)


E2M1 = np.array([0.0, 0.5, 1.0, 1.5, 2.0, 3.0, 4.0, 6.0, -0.0, -0.5, -1.0, -1.5, -2.0, -3.0, -4.0, -6.0])


def pack_weight(w, fmt):
    k, n = w.shape
    w = f64(np.asarray(w, np.float32).astype(ml_dtypes.bfloat16)).reshape(k // 32, 32, n)
    amax = np.abs(w).max(1)
    if fmt == "e4m3":
        byte = np.frexp(amax)[1] - 1 + 127 - 7
    else:
        mant, ex = np.frexp(amax / 6.0)
        byte = np.where(mant > 0.5, ex, ex - 1) + 127
    byte = np.clip(np.where(amax > 0, byte, 1), 1, 254)
    scaled = (w * np.exp2(127.0 - byte)[:, None, :]).reshape(k, n).astype(np.float32)
    by_word = np.ascontiguousarray(scaled.reshape(k // 512, 128, 4, n).transpose(0, 1, 3, 2))
    if fmt == "e4m3":
        words = by_word.astype(ml_dtypes.float8_e4m3fn).view(np.uint8)
    else:
        c = by_word.astype(ml_dtypes.float4_e2m1fn).view(np.uint8) & 0xF
        words = (c[..., 0::2] | (c[..., 1::2] << 4)).reshape(k // 512, 128, 2 * n)
    return np.ascontiguousarray(words), np.ascontiguousarray(byte.astype(np.uint8).reshape(k // 512, 16, n))


def unpack_weight(words, scales, fmt):
    g, _, n = scales.shape
    words = np.ascontiguousarray(words).reshape(g, 128, n, -1)
    if fmt == "e4m3":
        vals = words.view(ml_dtypes.float8_e4m3fn).astype(np.float64)
    else:
        nib = np.empty((g, 128, n, 4), np.uint8)
        nib[..., 0::2] = words & 0xF
        nib[..., 1::2] = words >> 4
        vals = E2M1[nib]
    vals = vals * np.repeat(np.exp2(scales.astype(np.float64) - 127.0), 8, axis=1)[..., None]
    return vals.transpose(0, 1, 3, 2).reshape(g * 512, n)


def gelu(v):
    return 0.5 * v * (1.0 + np.tanh(np.sqrt(2.0 / np.pi) * (v + 0.044715 * v**3)))


def striped8(idx):
    return np.concatenate([v.reshape(-1, 16).T for v in idx]).astype(np.uint16)


def unstriped8(offs):
    return np.stack([offs[16 * g:16 * g + 16].T.reshape(-1) for g in range(8)]).astype(np.int64)


def heads(h, wgt, idx8):
    r = np.arange(h.shape[0])
    return wgt[r // 4 % 128] * h[r[:, None], idx8[r % 512 // 64]]


def put_heads(h, wgs, idx8, t2):
    r = np.arange(h.shape[0])
    page = np.zeros((h.shape[0], t2))
    page[r[:, None], idx8[r % 512 // 64]] = wgs[r // 4 % 128] * h
    return page


T, S, P, T2, K, H, N = 2048, 512, 512, 1024, 1536, 1024, 768


def setup_inputs():
    n = np.random.standard_normal
    s = mx_kscale(K)[:, None]
    u = mx_kscale(H)[:, None]
    d = {}
    d["tab_words"], d["tab_scales"] = pack_weight(n((K, T)) * s, "e4m3")
    d["offs"] = striped(np.random.permutation(T)[:S])
    d["w1"] = (n((K, H)) / K ** 0.5 / s).astype(np.float32)
    d["gain"] = np.exp(0.4 * n(H)).astype(np.float32)
    d["offs2"] = striped8(np.stack([np.random.permutation(T2)[:S] for _ in range(8)]))
    d["wgs"] = np.repeat(np.random.uniform(0.5, 2.0, (8, S)), 16, axis=0).astype(np.float32)
    d["offs3"] = striped8(np.stack([np.random.permutation(T2)[:P] for _ in range(8)]))
    d["wgt"] = np.repeat(np.random.uniform(0.5, 2.0, (8, P)), 16, axis=0).astype(np.float32)
    d["rock"] = n((H, P)).astype(np.float32)
    d["gz"] = (np.exp(0.3 * n(H)) * u[:, 0]).astype(np.float32)
    d["w2_words"], d["w2_scales"] = pack_weight(n((H, N)) / H ** 0.5 / u, "e2m1")
    d["b2"] = (0.5 * n(N)).astype(np.float32)
    return d


def reference(tab_words, tab_scales, offs, w1, gain, offs2, wgs, offs3, wgt, rock, gz, w2_words, w2_scales, b2):
    v = unpack_weight(tab_words, tab_scales, "e4m3")[:, unstriped(offs)]
    h = f64(gain)[:, None] * np.exp(mxq(f64(w1), 0, "e4m3").T @ v)
    page = put_heads(h, f64(wgs), unstriped8(offs2), T2)
    x = heads(page, f64(wgt), unstriped8(offs3))
    z = f64(gz)[:, None] * np.log(x + np.exp(f64(rock)))
    w2 = unpack_weight(w2_words, w2_scales, "e2m1")
    return (w2.T @ mxq(z, 0, "e4m3")) + f64(b2)[:, None]

@@ -1,0 +1,243 @@
+from contextlib import ExitStack
+
+import concourse.mybir as mybir
+from concourse.masks import make_identity
+
+T, S, M, T2, K, H, N = 2048, 512, 512, 1024, 1536, 1024, 768
+FLOPS = 2 * K * H * S + 2 * H * N * M
+
+F32 = mybir.dt.float32
+BF16 = mybir.dt.bfloat16
+I32 = mybir.dt.int32
+U32 = mybir.dt.uint32
+U16 = mybir.dt.uint16
+U8 = mybir.dt.uint8
+FP8X4 = mybir.dt.float8_e4m3fn_x4
+FP4X4 = mybir.dt.float4_e2m1fn_x4
+ACT = mybir.ActivationFunctionType
+ALU = mybir.AluOpType
+
+P = 128
+PACK = 4
+KP = P * PACK
+K_PASSES = K // KP
+H_PASSES = H // KP
+N_TILES = N // P
+M_TILES = M // P
+PAGES = 3
+SUM_BANK, BACK_BANK = 7, 6
+
+
+def tile_list_pyramid_void_scores_kernel(
+    tc, tab_words, tab_scales, offs, w1, gain, offs2, wgs, offs3, wgt, rock, gz, w2_words, w2_scales, b2, out
+):
+    nc = tc.nc
+    with ExitStack() as ctx:
+        keep = ctx.enter_context(tc.tile_pool(name="keep", bufs=1))
+        psum = ctx.enter_context(tc.psum_pool(name="psum", bufs=1))
+
+        def bank(n):
+            return psum.tile([P, 512], F32, name="bank%d" % n, tag="bank%d" % n)
+
+        def stage(n, shape, dtype, name):
+            return keep.tile(shape, dtype, name=name, tag="stage%d" % n, align_bytes=64)
+
+        list1 = keep.tile([P, S // 16], U16, name="list1")
+        list2 = keep.tile([P, S // 16], U16, name="list2")
+        list3 = keep.tile([P, M // 16], U16, name="list3")
+        w1_raw = [[keep.tile([P, PACK, KP], F32, name="w1_raw%d%d" % (b, a)) for a in range(K_PASSES)] for b in range(H_PASSES)]
+        w1_codes = [[keep.tile([P, KP], U32, name="w1_codes%d%d" % (b, a), align_bytes=64) for a in range(K_PASSES)] for b in range(H_PASSES)]
+        w1_scales = [[keep.tile([P, KP], U8, name="w1_scales%d%d" % (b, a), align_bytes=64) for a in range(K_PASSES)] for b in range(H_PASSES)]
+        tab_sb = [keep.tile([P, T], I32, name="tab%d" % a) for a in range(K_PASSES)]
+        tab_sc = keep.tile([P, T], U8, name="tab_sc")
+        v_codes = [keep.tile([P, S], U32, name="v_codes%d" % a, align_bytes=64) for a in range(K_PASSES)]
+        v_scales = keep.tile([P, S], U8, name="v_scales", align_bytes=64)
+        gain_sb = keep.tile([P, H_PASSES, PACK], F32, name="gain_sb")
+        ln_gain = [keep.tile([P, PACK], F32, name="ln_gain0", tag="stage4", align_bytes=64), keep.tile([P, PACK], F32, name="ln_gain1")]
+        gz_sb = keep.tile([P, H_PASSES, PACK], F32, name="gz_sb")
+        b2_sb = keep.tile([P, N_TILES], F32, name="b2_sb")
+        wgs_sb = keep.tile([P, S], F32, name="wgs_sb")
+        wgt_sb = keep.tile([P, M], F32, name="wgt_sb")
+        rock_sb = [keep.tile([P, PACK, M], F32, name="rock%d" % b) for b in range(H_PASSES)]
+        w2_sb = keep.tile([P, H_PASSES, 2 * N], U8, name="w2_sb", align_bytes=64)
+        w2_sc = keep.tile([P, H_PASSES, N], U8, name="w2_sc", align_bytes=64)
+        pages = [keep.tile([P, T2], F32, name="page%d" % n) for n in range(PAGES)]
+        h = [[keep.tile([P, S], F32, name="h%d%d" % (b, i)) for i in range(PACK)] for b in range(H_PASSES)]
+        z_codes = [keep.tile([P, M], U32, name="z_codes%d" % b, align_bytes=64) for b in range(H_PASSES)]
+        ident = keep.tile([P, P], F32, name="ident", tag="ident", align_bytes=64)
+
+        nc.vector.memset(tab_sc[:].bitcast(I32), 0)
+        nc.vector.memset(w2_sc[:].rearrange("p b n -> p (b n)").bitcast(I32), 0)
+        for page in pages:
+            nc.vector.memset(page[:], 0.0)
+        make_identity(nc, ident[:])
+
+        def load_w1(b, a):
+            rows = w1[a * KP : (a + 1) * KP, b * KP : (b + 1) * KP]
+            nc.sync.dma_start(out=w1_raw[b][a][:], in_=rows.rearrange("(p j) r -> p j r", j=PACK))
+
+        def load_tab(a):
+            nc.sync.dma_start(out=tab_sb[a][:], in_=tab_words[a].rearrange("p t i -> p (t i)").bitcast(I32))
+
+        nc.sync.dma_start(list1[:], offs)
+        load_w1(0, 0)
+        nc.scalar.dma_start(out=gain_sb[:], in_=gain.rearrange("(b p i) -> p b i", p=P, i=PACK))
+        nc.scalar.dma_start(out=gz_sb[:], in_=gz.rearrange("(b p i) -> p b i", p=P, i=PACK))
+        with nc.allow_non_contiguous_dma(reason="one bias value for each partition"):
+            nc.scalar.dma_start(out=b2_sb[:], in_=b2.rearrange("(c p) -> p c", p=P))
+        nc.sync.dma_start(list2[:], offs2)
+        nc.sync.dma_start(list3[:], offs3)
+        load_w1(0, 1)
+        for q in range(4):
+            nc.sync.dma_start(
+                out=tab_sc[32 * q : 32 * q + 4 * K_PASSES, :].bitcast(I32),
+                in_=tab_scales[:, 4 * q : 4 * q + 4, :].bitcast(I32),
+            )
+        load_w1(0, 2)
+        for a in range(K_PASSES):
+            load_tab(a)
+        nc.sync.dma_start(out=wgs_sb[:], in_=wgs)
+        for a in range(K_PASSES):
+            load_w1(1, a)
+        nc.sync.dma_start(out=wgt_sb[:], in_=wgt)
+        for b in reversed(range(H_PASSES)):
+            nc.sync.dma_start(out=rock_sb[b][:], in_=rock[b * KP : (b + 1) * KP, :].rearrange("(p i) m -> p i m", i=PACK))
+        nc.sync.dma_start(out=w2_sb[:].bitcast(I32), in_=w2_words.rearrange("b p c -> p b c").bitcast(I32))
+        for q in range(4):
+            nc.sync.dma_start(
+                out=w2_sc[32 * q : 32 * q + 4, :, :].bitcast(I32),
+                in_=w2_scales[:, 4 * q : 4 * q + 4, :].rearrange("b r n -> r b n").bitcast(I32),
+            )
+
+        for b in range(H_PASSES):
+            nc.scalar.activation(out=ln_gain[b][:], in_=gain_sb[:, b, :], func=ACT.Ln)
+
+        def quantize_w1(b, a):
+            grouped = stage(4 if (b, a) == (1, 0) else a, [P, PACK, P, PACK], BF16, "w1_grouped%d%d" % (b, a))
+            copy = nc.vector.tensor_copy if (b, a) == (0, 0) else nc.scalar.copy
+            copy(
+                out=grouped[:].rearrange("p t m j -> p m j t"),
+                in_=w1_raw[b][a][:].rearrange("p j (m t) -> p m j t", t=PACK),
+            )
+            nc.vector.quantize_mx(
+                out=w1_codes[b][a][:].bitcast(FP8X4),
+                scales=w1_scales[b][a][:],
+                in_=grouped[:].rearrange("p t m j -> p (t m j)"),
+            )
+
+        def first_product(b):
+            acc = [bank(PACK * b + i) for i in range(PACK)]
+            for a in range(K_PASSES):
+                for i in range(PACK):
+                    cols = slice(i * P, (i + 1) * P)
+                    nc.tensor.matmul_mx(
+                        out=acc[i][:],
+                        lhsT=w1_codes[b][a][:, cols].bitcast(FP8X4),
+                        lhsT_scale=w1_scales[b][a][:, cols],
+                        rhs=v_codes[a][:].bitcast(FP8X4),
+                        rhs_scale=v_scales[4 * a :, :],
+                        start=(a == 0),
+                        stop=(a == K_PASSES - 1),
+                    )
+            for i in range(PACK):
+                nc.scalar.activation(out=h[b][i][:], in_=acc[i][:], func=ACT.Exp, bias=ln_gain[b][:, i : i + 1])
+
+        nc.vector.tensor_copy(v_scales[:], tab_sc[:].indirect(list1[:]))
+        for a in range(K_PASSES):
+            quantize_w1(0, a)
+            nc.vector.tensor_copy(v_codes[a][:], tab_sb[a][:].bitcast(U32).indirect(list1[:]))
+        first_product(0)
+        for a in range(K_PASSES):
+            quantize_w1(1, a)
+        first_product(1)
+        for b in reversed(range(H_PASSES)):
+            nc.scalar.activation(out=rock_sb[b][:], in_=rock_sb[b][:], func=ACT.Exp)
+
+        tiles = H_PASSES * PACK
+        last = tiles - 1
+        page_of = [pages[t % PAGES] for t in range(last)] + [pages[(last - 2) % PAGES]]
+
+        def scatter(t):
+            b, i = divmod(t, PACK)
+            nc.vector.tensor_tensor(page_of[t][:].indirect(list2[:]), h[b][i][:], wgs_sb[:], ALU.mult)
+
+        def gather(t, x):
+            nc.vector.tensor_tensor(x, page_of[t][:].indirect(list3[:]), wgt_sb[:], ALU.mult)
+
+        def logs_tile(t):
+            n = min(t, last - 1) % 2
+            return keep.tile([P, M], F32, name="logs%d" % t, tag="logs%d" % n)
+
+        def log_plane(t, x, grouped):
+            b, i = divmod(t, PACK)
+            total = bank(SUM_BANK - 2 * (t % 2))
+            terms = [rock_sb[b][:, i, :], x]
+            for n, term in enumerate(terms):
+                for c in range(M_TILES):
+                    cols = slice(c * P, (c + 1) * P)
+                    nc.tensor.matmul(
+                        total[:, cols], term[:, cols], ident[:], is_transpose=True,
+                        start=(n == 0 and c == 0), stop=(n == len(terms) - 1 and c == M_TILES - 1),
+                    )
+            logs = logs_tile(t)
+            nc.scalar.activation(out=logs[:], in_=total[:], func=ACT.Ln)
+            back = bank(BACK_BANK - 2 * (t % 2))
+            for c in range(M_TILES):
+                cols = slice(c * P, (c + 1) * P)
+                nc.tensor.transpose(back[:, cols], logs[:, cols], ident[:])
+            nc.scalar.activation(out=grouped[:, :, i], in_=back[:], func=ACT.Copy, scale=gz_sb[:, b, i : i + 1])
+
+        def quantize_z(b, grouped, scales):
+            nc.vector.quantize_mx(
+                out=z_codes[b][:].bitcast(FP8X4), scales=scales[:], in_=grouped[:].rearrange("p m i -> p (m i)")
+            )
+
+        def second_product(b, n, acc, scales):
+            nc.tensor.matmul_mx(
+                out=acc[:],
+                lhsT=w2_sb[:, b, 2 * n * P : 2 * (n + 1) * P].bitcast(FP4X4),
+                lhsT_scale=w2_sc[:, b, n * P : (n + 1) * P],
+                rhs=z_codes[b][:].bitcast(FP8X4),
+                rhs_scale=scales[:],
+                start=(b == 0),
+                stop=(b == H_PASSES - 1),
+            )
+
+        x_stage = [2, 1, 0, 2]
+        z_stage = [3, 1]
+        z_grouped = []
+        scatter(0)
+        xs = None
+        for t in range(tiles):
+            b, i = divmod(t, PACK)
+            if t + 1 < last:
+                scatter(t + 1)
+            if t == last:
+                scatter(last)
+            if t % 2 == 0:
+                xs = stage(x_stage[t // 2], [P, 2, M], F32, "x%d" % t)
+            gather(t, xs[:, t % 2, :])
+            if i == 0:
+                z_grouped.append(stage(z_stage[b], [P, M, PACK], BF16, "z_grouped%d" % b))
+            if t < last:
+                log_plane(t, xs[:, t % 2, :], z_grouped[b])
+        total = keep.tile([P, M], F32, name="total")
+        nc.vector.tensor_tensor(total[:], xs[:, 1, :], rock_sb[1][:, PACK - 1, :], ALU.add)
+        logs = logs_tile(last)
+        nc.scalar.activation(out=logs[:], in_=total[:], func=ACT.Ln)
+        z_scales0 = keep.tile([P, M], U8, name="z_scales0", tag="ident", align_bytes=64)
+        quantize_z(0, z_grouped[0], z_scales0)
+        acc2 = [bank(n) for n in range(N_TILES)]
+        for n in range(N_TILES):
+            second_product(0, n, acc2[n], z_scales0)
+        nc.vector.tensor_scalar(z_grouped[1][:, :, PACK - 1], logs[:], gz_sb[:, 1, PACK - 1 : PACK], None, ALU.mult)
+        z_scales1 = keep.tile([P, M], U8, name="z_scales1", align_bytes=64)
+        quantize_z(1, z_grouped[1], z_scales1)
+        for n in range(N_TILES):
+            second_product(1, n, acc2[n], z_scales1)
+            result = keep.tile([P, M], F32, name="result%d" % n)
+            if n % 2 == 0:
+                nc.scalar.activation(out=result[:], in_=acc2[n][:], func=ACT.Identity, bias=b2_sb[:, n : n + 1])
+            else:
+                nc.vector.tensor_scalar(result[:], acc2[n][:], b2_sb[:, n : n + 1], None, ALU.add)
+            nc.sync.dma_start(out=out[n * P : (n + 1) * P, :], in_=result[:])

@@ -24,6 +24,7 @@ K_PASSES = K // KP
 H_PASSES = H // KP
 N_TILES = N // P
 M_TILES = M // P
+HALF = 256
 PAGES = 3
 SUM_BANK, BACK_BANK = 7, 6
 
@@ -46,15 +47,15 @@ def tile_list_pyramid_void_scores_kernel(
         list2 = keep.tile([P, S // 16], U16, name="list2")
         list3 = keep.tile([P, M // 16], U16, name="list3")
         w1_raw = [[keep.tile([P, PACK, KP], F32, name="w1_raw%d%d" % (b, a)) for a in range(K_PASSES)] for b in range(H_PASSES)]
-        w1_codes = [[keep.tile([P, KP], U32, name="w1_codes%d%d" % (b, a), align_bytes=64) for a in range(K_PASSES)] for b in range(H_PASSES)]
+        w1_codes = {}
         w1_scales = [[keep.tile([P, KP], U8, name="w1_scales%d%d" % (b, a), align_bytes=64) for a in range(K_PASSES)] for b in range(H_PASSES)]
-        tab_sb = [keep.tile([P, T], I32, name="tab%d" % a) for a in range(K_PASSES)]
+        tab_sb = [keep.tile([P, T], I32, name="tab%d" % a, tag="tab%d" % a, align_bytes=64) for a in range(K_PASSES)]
         tab_sc = keep.tile([P, T], U8, name="tab_sc")
         v_codes = [keep.tile([P, S], U32, name="v_codes%d" % a, align_bytes=64) for a in range(K_PASSES)]
         v_scales = keep.tile([P, S], U8, name="v_scales", align_bytes=64)
         gain_sb = keep.tile([P, H_PASSES, PACK], F32, name="gain_sb")
         ln_gain = [keep.tile([P, PACK], F32, name="ln_gain0", tag="stage4", align_bytes=64), keep.tile([P, PACK], F32, name="ln_gain1")]
-        gz_sb = keep.tile([P, H_PASSES, PACK], F32, name="gz_sb")
+        gz_sb = [keep.tile([P, PACK], F32, name="gz%d" % b) for b in range(H_PASSES)]
         b2_sb = keep.tile([P, N_TILES], F32, name="b2_sb")
         wgs_sb = keep.tile([P, S], F32, name="wgs_sb")
         wgt_sb = keep.tile([P, M], F32, name="wgt_sb")
@@ -79,21 +80,21 @@ def tile_list_pyramid_void_scores_kernel(
         def load_tab(a):
             nc.sync.dma_start(out=tab_sb[a][:], in_=tab_words[a].rearrange("p t i -> p (t i)").bitcast(I32))
 
+        gz_rows = gz.rearrange("(b p i) -> p b i", p=P, i=PACK)
         nc.sync.dma_start(list1[:], offs)
         load_w1(0, 0)
-        nc.scalar.dma_start(out=gain_sb[:], in_=gain.rearrange("(b p i) -> p b i", p=P, i=PACK))
-        nc.scalar.dma_start(out=gz_sb[:], in_=gz.rearrange("(b p i) -> p b i", p=P, i=PACK))
-        with nc.allow_non_contiguous_dma(reason="one bias value for each partition"):
-            nc.scalar.dma_start(out=b2_sb[:], in_=b2.rearrange("(c p) -> p c", p=P))
+        nc.sync.dma_start(out=gain_sb[:], in_=gain.rearrange("(b p i) -> p b i", p=P, i=PACK))
         nc.sync.dma_start(list2[:], offs2)
+        nc.sync.dma_start(out=gz_sb[0][:], in_=gz_rows[:, 0, :])
         nc.sync.dma_start(list3[:], offs3)
         load_w1(0, 1)
+        load_w1(0, 2)
+        nc.sync.dma_start(out=gz_sb[1][:], in_=gz_rows[:, 1, :])
         for q in range(4):
             nc.sync.dma_start(
                 out=tab_sc[32 * q : 32 * q + 4 * K_PASSES, :].bitcast(I32),
                 in_=tab_scales[:, 4 * q : 4 * q + 4, :].bitcast(I32),
             )
-        load_w1(0, 2)
         for a in range(K_PASSES):
             load_tab(a)
         nc.sync.dma_start(out=wgs_sb[:], in_=wgs)
@@ -108,9 +109,13 @@ def tile_list_pyramid_void_scores_kernel(
                 out=w2_sc[32 * q : 32 * q + 4, :, :].bitcast(I32),
                 in_=w2_scales[:, 4 * q : 4 * q + 4, :].rearrange("b r n -> r b n").bitcast(I32),
             )
+        with nc.allow_non_contiguous_dma(reason="one bias value for each partition"):
+            nc.sync.dma_start(out=b2_sb[:], in_=b2.rearrange("(c p) -> p c", p=P))
 
         for b in range(H_PASSES):
             nc.scalar.activation(out=ln_gain[b][:], in_=gain_sb[:, b, :], func=ACT.Ln)
+        warm = keep.tile([P, 1], F32, name="warm")
+        nc.scalar.activation(out=warm[:], in_=ln_gain[1][:, 0:1], func=ACT.Exp)
 
         def quantize_w1(b, a):
             grouped = stage(4 if (b, a) == (1, 0) else a, [P, PACK, P, PACK], BF16, "w1_grouped%d%d" % (b, a))
@@ -119,33 +124,49 @@ def tile_list_pyramid_void_scores_kernel(
                 out=grouped[:].rearrange("p t m j -> p m j t"),
                 in_=w1_raw[b][a][:].rearrange("p j (m t) -> p m j t", t=PACK),
             )
+            tag = "tab0" if (b, a) == (0, K_PASSES - 1) else "w1_codes%d%d" % (b, a)
+            w1_codes[b, a] = keep.tile([P, KP], U32, name="w1_codes%d%d" % (b, a), tag=tag, align_bytes=64)
             nc.vector.quantize_mx(
-                out=w1_codes[b][a][:].bitcast(FP8X4),
+                out=w1_codes[b, a][:].bitcast(FP8X4),
                 scales=w1_scales[b][a][:],
                 in_=grouped[:].rearrange("p t m j -> p (t m j)"),
             )
 
+        halves = [slice(0, HALF), slice(HALF, 2 * HALF)]
+        list_halves = [slice(0, HALF // 16), slice(HALF // 16, 2 * HALF // 16)]
+        whole = slice(0, 2 * HALF)
+
         def first_product(b):
-            acc = [bank(PACK * b + i) for i in range(PACK)]
-            for a in range(K_PASSES):
-                for i in range(PACK):
+            pieces = [(i, whole, bank(PACK * b + i)) for i in range(PACK)]
+            if b == 0:
+                pieces = [(0, halves[0], pieces[0][2]), (0, halves[1], bank(PACK))] + pieces[1:]
+            order = [(a, piece) for a in range(K_PASSES) for piece in pieces]
+            if b == 0:
+                order = [(a, piece) for piece in pieces for a in range(K_PASSES)]
+            if True:
+                for a, (i, js, acc) in order:
                     cols = slice(i * P, (i + 1) * P)
                     nc.tensor.matmul_mx(
-                        out=acc[i][:],
-                        lhsT=w1_codes[b][a][:, cols].bitcast(FP8X4),
+                        out=acc[:, js],
+                        lhsT=w1_codes[b, a][:, cols].bitcast(FP8X4),
                         lhsT_scale=w1_scales[b][a][:, cols],
-                        rhs=v_codes[a][:].bitcast(FP8X4),
-                        rhs_scale=v_scales[4 * a :, :],
+                        rhs=v_codes[a][:, js].bitcast(FP8X4),
+                        rhs_scale=v_scales[4 * a :, js],
                         start=(a == 0),
                         stop=(a == K_PASSES - 1),
                     )
-            for i in range(PACK):
-                nc.scalar.activation(out=h[b][i][:], in_=acc[i][:], func=ACT.Exp, bias=ln_gain[b][:, i : i + 1])
+            for i, js, acc in pieces:
+                nc.scalar.activation(out=h[b][i][:, js], in_=acc[:, js], func=ACT.Exp, bias=ln_gain[b][:, i : i + 1])
 
         nc.vector.tensor_copy(v_scales[:], tab_sc[:].indirect(list1[:]))
-        for a in range(K_PASSES):
+        for a in range(K_PASSES - 1):
             quantize_w1(0, a)
+        for a in range(K_PASSES - 1):
             nc.vector.tensor_copy(v_codes[a][:], tab_sb[a][:].bitcast(U32).indirect(list1[:]))
+            if a == 0:
+                quantize_w1(0, K_PASSES - 1)
+        for js, ls in zip(halves, list_halves):
+            nc.vector.tensor_copy(v_codes[-1][:, js], tab_sb[-1][:].bitcast(U32).indirect(list1[:, ls]))
         first_product(0)
         for a in range(K_PASSES):
             quantize_w1(1, a)
@@ -157,12 +178,12 @@ def tile_list_pyramid_void_scores_kernel(
         last = tiles - 1
         page_of = [pages[t % PAGES] for t in range(last)] + [pages[(last - 2) % PAGES]]
 
-        def scatter(t):
+        def scatter(t, js=whole, ls=slice(0, S // 16)):
             b, i = divmod(t, PACK)
-            nc.vector.tensor_tensor(page_of[t][:].indirect(list2[:]), h[b][i][:], wgs_sb[:], ALU.mult)
+            nc.vector.tensor_tensor(page_of[t][:].indirect(list2[:, ls]), h[b][i][:, js], wgs_sb[:, js], ALU.mult)
 
-        def gather(t, x):
-            nc.vector.tensor_tensor(x, page_of[t][:].indirect(list3[:]), wgt_sb[:], ALU.mult)
+        def gather(t, x, ms=whole, ls=slice(0, M // 16)):
+            nc.vector.tensor_tensor(x, page_of[t][:].indirect(list3[:, ls]), wgt_sb[:, ms], ALU.mult)
 
         def logs_tile(t):
             n = min(t, last - 1) % 2
@@ -185,59 +206,78 @@ def tile_list_pyramid_void_scores_kernel(
             for c in range(M_TILES):
                 cols = slice(c * P, (c + 1) * P)
                 nc.tensor.transpose(back[:, cols], logs[:, cols], ident[:])
-            nc.scalar.activation(out=grouped[:, :, i], in_=back[:], func=ACT.Copy, scale=gz_sb[:, b, i : i + 1])
+            nc.scalar.activation(out=grouped[:, :, i], in_=back[:], func=ACT.Copy, scale=gz_sb[b][:, i : i + 1])
 
-        def quantize_z(b, grouped, scales):
+        def quantize_z(b, grouped, scales, ms):
             nc.vector.quantize_mx(
-                out=z_codes[b][:].bitcast(FP8X4), scales=scales[:], in_=grouped[:].rearrange("p m i -> p (m i)")
+                out=z_codes[b][:, ms].bitcast(FP8X4),
+                scales=scales[:, ms],
+                in_=grouped[:, ms, :].rearrange("p m i -> p (m i)"),
             )
 
-        def second_product(b, n, acc, scales):
-            nc.tensor.matmul_mx(
-                out=acc[:],
-                lhsT=w2_sb[:, b, 2 * n * P : 2 * (n + 1) * P].bitcast(FP4X4),
-                lhsT_scale=w2_sc[:, b, n * P : (n + 1) * P],
-                rhs=z_codes[b][:].bitcast(FP8X4),
-                rhs_scale=scales[:],
-                start=(b == 0),
-                stop=(b == H_PASSES - 1),
-            )
+        def second_product(b, half, scales):
+            for pair in range(N_TILES // 2):
+                for j in range(2):
+                    n = 2 * pair + j
+                    for c in range(HALF // P):
+                        ms = slice(half * HALF + c * P, half * HALF + (c + 1) * P)
+                        nc.tensor.matmul_mx(
+                            out=acc2[half][pair][:, j * HALF + c * P : j * HALF + (c + 1) * P],
+                            lhsT=w2_sb[:, b, 2 * n * P : 2 * (n + 1) * P].bitcast(FP4X4),
+                            lhsT_scale=w2_sc[:, b, n * P : (n + 1) * P],
+                            rhs=z_codes[b][:, ms].bitcast(FP8X4),
+                            rhs_scale=scales[:, ms],
+                            start=(b == 0 and j == 0 and c == 0),
+                            stop=(b == H_PASSES - 1 and j == 1 and c == HALF // P - 1),
+                        )
 
         x_stage = [2, 1, 0, 2]
         z_stage = [3, 1]
         z_grouped = []
-        scatter(0)
+        for js, ls in zip(halves, list_halves):
+            scatter(0, js, ls)
         xs = None
-        for t in range(tiles):
+        for t in range(last):
             b, i = divmod(t, PACK)
             if t + 1 < last:
                 scatter(t + 1)
-            if t == last:
-                scatter(last)
             if t % 2 == 0:
                 xs = stage(x_stage[t // 2], [P, 2, M], F32, "x%d" % t)
             gather(t, xs[:, t % 2, :])
             if i == 0:
                 z_grouped.append(stage(z_stage[b], [P, M, PACK], BF16, "z_grouped%d" % b))
-            if t < last:
-                log_plane(t, xs[:, t % 2, :], z_grouped[b])
+            log_plane(t, xs[:, t % 2, :], z_grouped[b])
+        scatter(last)
+        z_scales = [
+            keep.tile([P, M], U8, name="z_scales0", tag="ident", align_bytes=64),
+            keep.tile([P, M], U8, name="z_scales1", align_bytes=64),
+        ]
+        quantize_z(0, z_grouped[0], z_scales[0], whole)
+        acc2 = [[bank(3 * half + pair) for pair in range(N_TILES // 2)] for half in range(2)]
+        for half in range(2):
+            second_product(0, half, z_scales[0])
+        x_last = stage(z_stage[0], [P, M], F32, "x_last")
         total = keep.tile([P, M], F32, name="total")
-        nc.vector.tensor_tensor(total[:], xs[:, 1, :], rock_sb[1][:, PACK - 1, :], ALU.add)
         logs = logs_tile(last)
-        nc.scalar.activation(out=logs[:], in_=total[:], func=ACT.Ln)
-        z_scales0 = keep.tile([P, M], U8, name="z_scales0", tag="ident", align_bytes=64)
-        quantize_z(0, z_grouped[0], z_scales0)
-        acc2 = [bank(n) for n in range(N_TILES)]
-        for n in range(N_TILES):
-            second_product(0, n, acc2[n], z_scales0)
-        nc.vector.tensor_scalar(z_grouped[1][:, :, PACK - 1], logs[:], gz_sb[:, 1, PACK - 1 : PACK], None, ALU.mult)
-        z_scales1 = keep.tile([P, M], U8, name="z_scales1", align_bytes=64)
-        quantize_z(1, z_grouped[1], z_scales1)
-        for n in range(N_TILES):
-            second_product(1, n, acc2[n], z_scales1)
-            result = keep.tile([P, M], F32, name="result%d" % n)
-            if n % 2 == 0:
-                nc.scalar.activation(out=result[:], in_=acc2[n][:], func=ACT.Identity, bias=b2_sb[:, n : n + 1])
-            else:
-                nc.vector.tensor_scalar(result[:], acc2[n][:], b2_sb[:, n : n + 1], None, ALU.add)
-            nc.sync.dma_start(out=out[n * P : (n + 1) * P, :], in_=result[:])
+        for ms, ls in zip(halves, list_halves):
+            gather(last, x_last[:, ms], ms, ls)
+        for ms in halves:
+            nc.vector.tensor_tensor(total[:, ms], x_last[:, ms], rock_sb[1][:, PACK - 1, ms], ALU.add)
+            nc.scalar.activation(out=logs[:, ms], in_=total[:, ms], func=ACT.Ln)
+        for ms in halves:
+            nc.vector.tensor_scalar(z_grouped[1][:, ms, PACK - 1], logs[:, ms], gz_sb[1][:, PACK - 1 : PACK], None, ALU.mult)
+        for half in range(2):
+            quantize_z(1, z_grouped[1], z_scales[1], halves[half])
+            second_product(1, half, z_scales[1])
+        for half in range(2):
+            for pair in range(N_TILES // 2):
+                result = keep.tile([P, 2, HALF], F32, name="result%d%d" % (half, pair))
+                for j in range(2):
+                    n = 2 * pair + j
+                    sums = acc2[half][pair][:, j * HALF : (j + 1) * HALF]
+                    if (3 * half + pair) % 2 == 0:
+                        nc.scalar.activation(out=result[:, j, :], in_=sums, func=ACT.Identity, bias=b2_sb[:, n : n + 1])
+                    else:
+                        nc.vector.tensor_scalar(result[:, j, :], sums, b2_sb[:, n : n + 1], None, ALU.add)
+                rows = out[2 * pair * P : 2 * (pair + 1) * P, halves[half]]
+                nc.sync.dma_start(out=rows.rearrange("(j p) m -> p j m", p=P), in_=result[:])

@@ -63,7 +63,7 @@ def tile_list_pyramid_void_scores_kernel(
         w2_sb = keep.tile([P, H_PASSES, 2 * N], U8, name="w2_sb", align_bytes=64)
         w2_sc = keep.tile([P, H_PASSES, N], U8, name="w2_sc", align_bytes=64)
         pages = [keep.tile([P, T2], F32, name="page%d" % n) for n in range(PAGES)]
-        h = [[keep.tile([P, S], F32, name="h%d%d" % (b, i)) for i in range(PACK)] for b in range(H_PASSES)]
+        h = [[keep.tile([P, S], F32, name="h%d%d" % (b, i), tag="h%d%d" % (b, i)) for i in range(PACK)] for b in range(H_PASSES)]
         z_codes = [keep.tile([P, M], U32, name="z_codes%d" % b, align_bytes=64) for b in range(H_PASSES)]
         ident = keep.tile([P, P], F32, name="ident", tag="ident", align_bytes=64)
 
@@ -121,8 +121,8 @@ def tile_list_pyramid_void_scores_kernel(
             grouped = stage(4 if (b, a) == (1, 0) else a, [P, PACK, P, PACK], BF16, "w1_grouped%d%d" % (b, a))
             copy = nc.vector.tensor_copy if (b, a) == (0, 0) else nc.scalar.copy
             copy(
-                out=grouped[:].rearrange("p t m j -> p m j t"),
-                in_=w1_raw[b][a][:].rearrange("p j (m t) -> p m j t", t=PACK),
+                out=grouped[:].rearrange("p t m j -> p m t j"),
+                in_=w1_raw[b][a][:].rearrange("p j (m t) -> p m t j", t=PACK),
             )
             tag = "tab0" if (b, a) == (0, K_PASSES - 1) else "w1_codes%d%d" % (b, a)
             w1_codes[b, a] = keep.tile([P, KP], U32, name="w1_codes%d%d" % (b, a), tag=tag, align_bytes=64)
@@ -186,7 +186,7 @@ def tile_list_pyramid_void_scores_kernel(
             nc.vector.tensor_tensor(x, page_of[t][:].indirect(list3[:, ls]), wgt_sb[:, ms], ALU.mult)
 
         def logs_tile(t):
-            n = min(t, last - 1) % 2
+            n = t % 2 if t <= PACK else (t - PACK) // 2
             return keep.tile([P, M], F32, name="logs%d" % t, tag="logs%d" % n)
 
         def log_plane(t, x, grouped):
@@ -231,7 +231,7 @@ def tile_list_pyramid_void_scores_kernel(
                             stop=(b == H_PASSES - 1 and j == 1 and c == HALF // P - 1),
                         )
 
-        x_stage = [2, 1, 0, 2]
+        x_stage = [2, 1, 0, 5]
         z_stage = [3, 1]
         z_grouped = []
         for js, ls in zip(halves, list_halves):
@@ -243,10 +243,13 @@ def tile_list_pyramid_void_scores_kernel(
                 scatter(t + 1)
             if t % 2 == 0:
                 xs = stage(x_stage[t // 2], [P, 2, M], F32, "x%d" % t)
-            gather(t, xs[:, t % 2, :])
+            x = xs[:, t % 2, :]
+            if t == last - 2:
+                x = keep.tile([P, M], F32, name="x5", tag="h12")[:]
+            gather(t, x)
             if i == 0:
                 z_grouped.append(stage(z_stage[b], [P, M, PACK], BF16, "z_grouped%d" % b))
-            log_plane(t, xs[:, t % 2, :], z_grouped[b])
+            log_plane(t, x, z_grouped[b])
         scatter(last)
         z_scales = [
             keep.tile([P, M], U8, name="z_scales0", tag="ident", align_bytes=64),

@@ -22,10 +22,19 @@ PACK = 4
 KP = P * PACK
 K_PASSES = K // KP
 H_PASSES = H // KP
+ROW_TILES = H_PASSES * PACK
+LAST = ROW_TILES - 1
 N_TILES = N // P
 M_TILES = M // P
+QUADRANTS = 4
+SCALE_ROWS = 4
+BANK = 512
 HALF = 256
-PAGES = 3
+HALVES = [slice(0, HALF), slice(HALF, 2 * HALF)]
+LIST_HALVES = [slice(0, HALF // 16), slice(HALF // 16, 2 * HALF // 16)]
+WHOLE = slice(0, 2 * HALF)
+WHOLE_LIST = slice(0, 2 * HALF // 16)
+PAGES = PACK
 SUM_BANK, BACK_BANK = 7, 6
 
 
@@ -37,35 +46,35 @@ def tile_list_pyramid_void_scores_kernel(
         keep = ctx.enter_context(tc.tile_pool(name="keep", bufs=1))
         psum = ctx.enter_context(tc.psum_pool(name="psum", bufs=1))
 
-        def bank(n):
-            return psum.tile([P, 512], F32, name="bank%d" % n, tag="bank%d" % n)
+        def bank(number):
+            return psum.tile([P, BANK], F32, name="bank%d" % number, tag="bank%d" % number)
 
-        def stage(n, shape, dtype, name):
-            return keep.tile(shape, dtype, name=name, tag="stage%d" % n, align_bytes=64)
+        def new_tile(shape, dtype, name, tag=None):
+            return keep.tile(shape, dtype, name=name, tag=tag or name, align_bytes=64)
 
-        list1 = keep.tile([P, S // 16], U16, name="list1")
-        list2 = keep.tile([P, S // 16], U16, name="list2")
-        list3 = keep.tile([P, M // 16], U16, name="list3")
-        w1_raw = [[keep.tile([P, PACK, KP], F32, name="w1_raw%d%d" % (b, a)) for a in range(K_PASSES)] for b in range(H_PASSES)]
+        list1 = new_tile([P, S // 16], U16, "list1")
+        list2 = new_tile([P, S // 16], U16, "list2")
+        list3 = new_tile([P, M // 16], U16, "list3")
+        w1_raw = [[new_tile([P, PACK, KP], F32, "w1_raw%d%d" % (b, a)) for a in range(K_PASSES)] for b in range(H_PASSES)]
+        w1_scales = [[new_tile([P, KP], U8, "w1_scales%d%d" % (b, a)) for a in range(K_PASSES)] for b in range(H_PASSES)]
         w1_codes = {}
-        w1_scales = [[keep.tile([P, KP], U8, name="w1_scales%d%d" % (b, a), align_bytes=64) for a in range(K_PASSES)] for b in range(H_PASSES)]
-        tab_sb = [keep.tile([P, T], I32, name="tab%d" % a, tag="tab%d" % a, align_bytes=64) for a in range(K_PASSES)]
-        tab_sc = keep.tile([P, T], U8, name="tab_sc")
-        v_codes = [keep.tile([P, S], U32, name="v_codes%d" % a, align_bytes=64) for a in range(K_PASSES)]
-        v_scales = keep.tile([P, S], U8, name="v_scales", align_bytes=64)
-        gain_sb = keep.tile([P, H_PASSES, PACK], F32, name="gain_sb")
-        ln_gain = [keep.tile([P, PACK], F32, name="ln_gain0", tag="stage4", align_bytes=64), keep.tile([P, PACK], F32, name="ln_gain1")]
-        gz_sb = [keep.tile([P, PACK], F32, name="gz%d" % b) for b in range(H_PASSES)]
-        b2_sb = keep.tile([P, N_TILES], F32, name="b2_sb")
-        wgs_sb = keep.tile([P, S], F32, name="wgs_sb")
-        wgt_sb = keep.tile([P, M], F32, name="wgt_sb")
-        rock_sb = [keep.tile([P, PACK, M], F32, name="rock%d" % b) for b in range(H_PASSES)]
-        w2_sb = keep.tile([P, H_PASSES, 2 * N], U8, name="w2_sb", align_bytes=64)
-        w2_sc = keep.tile([P, H_PASSES, N], U8, name="w2_sc", align_bytes=64)
-        pages = [keep.tile([P, T2], F32, name="page%d" % n) for n in range(PAGES)]
-        h = [[keep.tile([P, S], F32, name="h%d%d" % (b, i), tag="h%d%d" % (b, i)) for i in range(PACK)] for b in range(H_PASSES)]
-        z_codes = [keep.tile([P, M], U32, name="z_codes%d" % b, align_bytes=64) for b in range(H_PASSES)]
-        ident = keep.tile([P, P], F32, name="ident", tag="ident", align_bytes=64)
+        tab_sb = [new_tile([P, T], I32, "tab%d" % a) for a in range(K_PASSES)]
+        tab_sc = new_tile([P, T], U8, "tab_sc")
+        v_codes = [new_tile([P, S], U32, "v_codes%d" % a) for a in range(K_PASSES)]
+        v_scales = new_tile([P, S], U8, "v_scales")
+        gain_sb = new_tile([P, H_PASSES, PACK], F32, "gain_sb")
+        ln_gain = [new_tile([P, PACK], F32, "ln_gain%d" % b) for b in range(H_PASSES)]
+        gz_sb = [new_tile([P, PACK], F32, "gz%d" % b) for b in range(H_PASSES)]
+        b2_sb = new_tile([P, N_TILES], F32, "b2_sb")
+        wgs_sb = new_tile([P, S], F32, "wgs_sb")
+        wgt_sb = new_tile([P, M], F32, "wgt_sb")
+        exp_rock = [new_tile([P, PACK, M], F32, "exp_rock%d" % b) for b in range(H_PASSES)]
+        w2_sb = new_tile([P, H_PASSES, 2 * N], U8, "w2_sb")
+        w2_sc = new_tile([P, H_PASSES, N], U8, "w2_sc")
+        pages = [new_tile([P, T2], F32, "page%d" % number) for number in range(PAGES)]
+        h = [new_tile([P, S], F32, "h%d" % t) for t in range(ROW_TILES)]
+        z_codes = [new_tile([P, M], U32, "z_codes%d" % b) for b in range(H_PASSES)]
+        ident = new_tile([P, P], F32, "ident")
 
         nc.vector.memset(tab_sc[:].bitcast(I32), 0)
         nc.vector.memset(w2_sc[:].rearrange("p b n -> p (b n)").bitcast(I32), 0)
@@ -77,9 +86,6 @@ def tile_list_pyramid_void_scores_kernel(
             rows = w1[a * KP : (a + 1) * KP, b * KP : (b + 1) * KP]
             nc.sync.dma_start(out=w1_raw[b][a][:], in_=rows.rearrange("(p j) r -> p j r", j=PACK))
 
-        def load_tab(a):
-            nc.sync.dma_start(out=tab_sb[a][:], in_=tab_words[a].rearrange("p t i -> p (t i)").bitcast(I32))
-
         gz_rows = gz.rearrange("(b p i) -> p b i", p=P, i=PACK)
         nc.sync.dma_start(list1[:], offs)
         load_w1(0, 0)
@@ -90,116 +96,112 @@ def tile_list_pyramid_void_scores_kernel(
         load_w1(0, 1)
         load_w1(0, 2)
         nc.sync.dma_start(out=gz_sb[1][:], in_=gz_rows[:, 1, :])
-        for q in range(4):
+        for q in range(QUADRANTS):
             nc.sync.dma_start(
-                out=tab_sc[32 * q : 32 * q + 4 * K_PASSES, :].bitcast(I32),
-                in_=tab_scales[:, 4 * q : 4 * q + 4, :].bitcast(I32),
+                out=tab_sc[32 * q : 32 * q + SCALE_ROWS * K_PASSES, :].bitcast(I32),
+                in_=tab_scales[:, SCALE_ROWS * q : SCALE_ROWS * (q + 1), :].bitcast(I32),
             )
         for a in range(K_PASSES):
-            load_tab(a)
+            nc.sync.dma_start(out=tab_sb[a][:], in_=tab_words[a].rearrange("p t i -> p (t i)").bitcast(I32))
         nc.sync.dma_start(out=wgs_sb[:], in_=wgs)
         for a in range(K_PASSES):
             load_w1(1, a)
         nc.sync.dma_start(out=wgt_sb[:], in_=wgt)
         for b in reversed(range(H_PASSES)):
-            nc.sync.dma_start(out=rock_sb[b][:], in_=rock[b * KP : (b + 1) * KP, :].rearrange("(p i) m -> p i m", i=PACK))
+            rows = rock[b * KP : (b + 1) * KP, :]
+            nc.sync.dma_start(out=exp_rock[b][:], in_=rows.rearrange("(p i) m -> p i m", i=PACK))
         nc.sync.dma_start(out=w2_sb[:].bitcast(I32), in_=w2_words.rearrange("b p c -> p b c").bitcast(I32))
-        for q in range(4):
+        for q in range(QUADRANTS):
             nc.sync.dma_start(
-                out=w2_sc[32 * q : 32 * q + 4, :, :].bitcast(I32),
-                in_=w2_scales[:, 4 * q : 4 * q + 4, :].rearrange("b r n -> r b n").bitcast(I32),
+                out=w2_sc[32 * q : 32 * q + SCALE_ROWS, :, :].bitcast(I32),
+                in_=w2_scales[:, SCALE_ROWS * q : SCALE_ROWS * (q + 1), :].rearrange("b s n -> s b n").bitcast(I32),
             )
         with nc.allow_non_contiguous_dma(reason="one bias value for each partition"):
-            nc.sync.dma_start(out=b2_sb[:], in_=b2.rearrange("(c p) -> p c", p=P))
+            nc.sync.dma_start(out=b2_sb[:], in_=b2.rearrange("(n p) -> p n", p=P))
 
         for b in range(H_PASSES):
             nc.scalar.activation(out=ln_gain[b][:], in_=gain_sb[:, b, :], func=ACT.Ln)
-        warm = keep.tile([P, 1], F32, name="warm")
-        nc.scalar.activation(out=warm[:], in_=ln_gain[1][:, 0:1], func=ACT.Exp)
+        warm_up = new_tile([P, 1], F32, "warm_up")
+        nc.scalar.activation(out=warm_up[:], in_=ln_gain[1][:, 0:1], func=ACT.Exp)
 
-        def quantize_w1(b, a):
-            grouped = stage(4 if (b, a) == (1, 0) else a, [P, PACK, P, PACK], BF16, "w1_grouped%d%d" % (b, a))
-            copy = nc.vector.tensor_copy if (b, a) == (0, 0) else nc.scalar.copy
+        def quantize_w1(b, a, copy=nc.scalar.copy, grouped_tag=None, codes_tag=None):
+            grouped = new_tile([P, PACK, P, PACK], BF16, "w1_grouped%d%d" % (b, a), grouped_tag or "stage%d" % a)
             copy(
-                out=grouped[:].rearrange("p t m j -> p m t j"),
-                in_=w1_raw[b][a][:].rearrange("p j (m t) -> p m t j", t=PACK),
+                out=grouped[:].rearrange("p i c j -> p c i j"),
+                in_=w1_raw[b][a][:].rearrange("p j (c i) -> p c i j", i=PACK),
             )
-            tag = "tab0" if (b, a) == (0, K_PASSES - 1) else "w1_codes%d%d" % (b, a)
-            w1_codes[b, a] = keep.tile([P, KP], U32, name="w1_codes%d%d" % (b, a), tag=tag, align_bytes=64)
+            w1_codes[b, a] = new_tile([P, KP], U32, "w1_codes%d%d" % (b, a), codes_tag)
             nc.vector.quantize_mx(
                 out=w1_codes[b, a][:].bitcast(FP8X4),
                 scales=w1_scales[b][a][:],
-                in_=grouped[:].rearrange("p t m j -> p (t m j)"),
+                in_=grouped[:].rearrange("p i c j -> p (i c j)"),
             )
 
-        halves = [slice(0, HALF), slice(HALF, 2 * HALF)]
-        list_halves = [slice(0, HALF // 16), slice(HALF // 16, 2 * HALF // 16)]
-        whole = slice(0, 2 * HALF)
+        def gather_words(a, js=WHOLE, ls=WHOLE_LIST):
+            nc.vector.tensor_copy(v_codes[a][:, js], tab_sb[a][:].bitcast(U32).indirect(list1[:, ls]))
 
-        def first_product(b):
-            pieces = [(i, whole, bank(PACK * b + i)) for i in range(PACK)]
-            if b == 0:
-                pieces = [(0, halves[0], pieces[0][2]), (0, halves[1], bank(PACK))] + pieces[1:]
-            order = [(a, piece) for a in range(K_PASSES) for piece in pieces]
-            if b == 0:
-                order = [(a, piece) for piece in pieces for a in range(K_PASSES)]
-            if True:
-                for a, (i, js, acc) in order:
-                    cols = slice(i * P, (i + 1) * P)
-                    nc.tensor.matmul_mx(
-                        out=acc[:, js],
-                        lhsT=w1_codes[b, a][:, cols].bitcast(FP8X4),
-                        lhsT_scale=w1_scales[b][a][:, cols],
-                        rhs=v_codes[a][:, js].bitcast(FP8X4),
-                        rhs_scale=v_scales[4 * a :, js],
-                        start=(a == 0),
-                        stop=(a == K_PASSES - 1),
-                    )
-            for i, js, acc in pieces:
-                nc.scalar.activation(out=h[b][i][:, js], in_=acc[:, js], func=ACT.Exp, bias=ln_gain[b][:, i : i + 1])
+        def first_product(b, work):
+            for a, i, js, acc in work:
+                cols = slice(i * P, (i + 1) * P)
+                nc.tensor.matmul_mx(
+                    out=acc[:, js],
+                    lhsT=w1_codes[b, a][:, cols].bitcast(FP8X4),
+                    lhsT_scale=w1_scales[b][a][:, cols],
+                    rhs=v_codes[a][:, js].bitcast(FP8X4),
+                    rhs_scale=v_scales[SCALE_ROWS * a :, js],
+                    start=(a == 0),
+                    stop=(a == K_PASSES - 1),
+                )
+            for a, i, js, acc in work:
+                if a == K_PASSES - 1:
+                    bias = ln_gain[b][:, i : i + 1]
+                    nc.scalar.activation(out=h[PACK * b + i][:, js], in_=acc[:, js], func=ACT.Exp, bias=bias)
 
         nc.vector.tensor_copy(v_scales[:], tab_sc[:].indirect(list1[:]))
-        for a in range(K_PASSES - 1):
-            quantize_w1(0, a)
-        for a in range(K_PASSES - 1):
-            nc.vector.tensor_copy(v_codes[a][:], tab_sb[a][:].bitcast(U32).indirect(list1[:]))
-            if a == 0:
-                quantize_w1(0, K_PASSES - 1)
-        for js, ls in zip(halves, list_halves):
-            nc.vector.tensor_copy(v_codes[-1][:, js], tab_sb[-1][:].bitcast(U32).indirect(list1[:, ls]))
-        first_product(0)
-        for a in range(K_PASSES):
-            quantize_w1(1, a)
-        first_product(1)
+        quantize_w1(0, 0, copy=nc.vector.tensor_copy)
+        quantize_w1(0, 1)
+        gather_words(0)
+        quantize_w1(0, 2, codes_tag="tab0")
+        gather_words(1)
+        for js, ls in zip(HALVES, LIST_HALVES):
+            gather_words(2, js, ls)
+        banks = [bank(i) for i in range(PACK)]
+        pieces = [(0, HALVES[0], banks[0]), (0, HALVES[1], bank(PACK))] + [(i, WHOLE, banks[i]) for i in range(1, PACK)]
+        first_product(0, [(a, i, js, acc) for i, js, acc in pieces for a in range(K_PASSES)])
+        quantize_w1(1, 0, grouped_tag="ln_gain0")
+        quantize_w1(1, 1)
+        quantize_w1(1, 2)
+        banks = [bank(PACK + i) for i in range(PACK)]
+        first_product(1, [(a, i, WHOLE, banks[i]) for a in range(K_PASSES) for i in range(PACK)])
         for b in reversed(range(H_PASSES)):
-            nc.scalar.activation(out=rock_sb[b][:], in_=rock_sb[b][:], func=ACT.Exp)
+            nc.scalar.activation(out=exp_rock[b][:], in_=exp_rock[b][:], func=ACT.Exp)
 
-        tiles = H_PASSES * PACK
-        last = tiles - 1
-        page_of = [pages[t % PAGES] for t in range(last)] + [pages[(last - 2) % PAGES]]
+        page_of = [pages[t % PAGES] for t in range(LAST)] + [pages[(LAST - 2) % PAGES]]
 
-        def scatter(t, js=whole, ls=slice(0, S // 16)):
-            b, i = divmod(t, PACK)
-            nc.vector.tensor_tensor(page_of[t][:].indirect(list2[:, ls]), h[b][i][:, js], wgs_sb[:, js], ALU.mult)
+        def scatter(t, js=WHOLE, ls=WHOLE_LIST):
+            nc.vector.tensor_tensor(page_of[t][:].indirect(list2[:, ls]), h[t][:, js], wgs_sb[:, js], ALU.mult)
 
-        def gather(t, x, ms=whole, ls=slice(0, M // 16)):
+        def gather(t, x, ms=WHOLE, ls=WHOLE_LIST):
             nc.vector.tensor_tensor(x, page_of[t][:].indirect(list3[:, ls]), wgt_sb[:, ms], ALU.mult)
 
         def logs_tile(t):
-            n = t % 2 if t <= PACK else (t - PACK) // 2
-            return keep.tile([P, M], F32, name="logs%d" % t, tag="logs%d" % n)
+            number = t % 2 if t <= PACK else (t - PACK) // 2
+            return new_tile([P, M], F32, "logs%d" % t, "logs%d" % number)
 
-        def log_plane(t, x, grouped):
+        def log_and_scale(t, x, grouped):
             b, i = divmod(t, PACK)
             total = bank(SUM_BANK - 2 * (t % 2))
-            terms = [rock_sb[b][:, i, :], x]
-            for n, term in enumerate(terms):
-                for c in range(M_TILES):
-                    cols = slice(c * P, (c + 1) * P)
-                    nc.tensor.matmul(
-                        total[:, cols], term[:, cols], ident[:], is_transpose=True,
-                        start=(n == 0 and c == 0), stop=(n == len(terms) - 1 and c == M_TILES - 1),
-                    )
+            blocks = [(term, c) for term in (exp_rock[b][:, i, :], x) for c in range(M_TILES)]
+            for number, (term, c) in enumerate(blocks):
+                cols = slice(c * P, (c + 1) * P)
+                nc.tensor.matmul(
+                    total[:, cols],
+                    term[:, cols],
+                    ident[:],
+                    is_transpose=True,
+                    start=(number == 0),
+                    stop=(number == len(blocks) - 1),
+                )
             logs = logs_tile(t)
             nc.scalar.activation(out=logs[:], in_=total[:], func=ACT.Ln)
             back = bank(BACK_BANK - 2 * (t % 2))
@@ -208,79 +210,79 @@ def tile_list_pyramid_void_scores_kernel(
                 nc.tensor.transpose(back[:, cols], logs[:, cols], ident[:])
             nc.scalar.activation(out=grouped[:, :, i], in_=back[:], func=ACT.Copy, scale=gz_sb[b][:, i : i + 1])
 
-        def quantize_z(b, grouped, scales, ms):
-            nc.vector.quantize_mx(
-                out=z_codes[b][:, ms].bitcast(FP8X4),
-                scales=scales[:, ms],
-                in_=grouped[:, ms, :].rearrange("p m i -> p (m i)"),
-            )
-
-        def second_product(b, half, scales):
-            for pair in range(N_TILES // 2):
-                for j in range(2):
-                    n = 2 * pair + j
-                    for c in range(HALF // P):
-                        ms = slice(half * HALF + c * P, half * HALF + (c + 1) * P)
-                        nc.tensor.matmul_mx(
-                            out=acc2[half][pair][:, j * HALF + c * P : j * HALF + (c + 1) * P],
-                            lhsT=w2_sb[:, b, 2 * n * P : 2 * (n + 1) * P].bitcast(FP4X4),
-                            lhsT_scale=w2_sc[:, b, n * P : (n + 1) * P],
-                            rhs=z_codes[b][:, ms].bitcast(FP8X4),
-                            rhs_scale=scales[:, ms],
-                            start=(b == 0 and j == 0 and c == 0),
-                            stop=(b == H_PASSES - 1 and j == 1 and c == HALF // P - 1),
-                        )
-
-        x_stage = [2, 1, 0, 5]
-        z_stage = [3, 1]
+        x_pair_tags = ["stage2", "stage1", "stage0", "x6"]
+        z_grouped_tags = ["z_grouped0", "stage1"]
         z_grouped = []
-        for js, ls in zip(halves, list_halves):
+        for js, ls in zip(HALVES, LIST_HALVES):
             scatter(0, js, ls)
-        xs = None
-        for t in range(last):
+        for t in range(LAST):
             b, i = divmod(t, PACK)
-            if t + 1 < last:
+            if t + 1 < LAST:
                 scatter(t + 1)
             if t % 2 == 0:
-                xs = stage(x_stage[t // 2], [P, 2, M], F32, "x%d" % t)
-            x = xs[:, t % 2, :]
-            if t == last - 2:
-                x = keep.tile([P, M], F32, name="x5", tag="h12")[:]
+                x_pair = new_tile([P, 2, M], F32, "x_pair%d" % t, x_pair_tags[t // 2])
+            x = new_tile([P, M], F32, "x5", "h%d" % (t + 1))[:] if t == LAST - 2 else x_pair[:, t % 2, :]
             gather(t, x)
             if i == 0:
-                z_grouped.append(stage(z_stage[b], [P, M, PACK], BF16, "z_grouped%d" % b))
-            log_plane(t, x, z_grouped[b])
-        scatter(last)
-        z_scales = [
-            keep.tile([P, M], U8, name="z_scales0", tag="ident", align_bytes=64),
-            keep.tile([P, M], U8, name="z_scales1", align_bytes=64),
-        ]
-        quantize_z(0, z_grouped[0], z_scales[0], whole)
-        acc2 = [[bank(3 * half + pair) for pair in range(N_TILES // 2)] for half in range(2)]
+                z_grouped.append(new_tile([P, M, PACK], BF16, "z_grouped%d" % b, z_grouped_tags[b]))
+            log_and_scale(t, x, z_grouped[b])
+        scatter(LAST)
+
+        z_scales = [new_tile([P, M], U8, "z_scales0", "ident"), new_tile([P, M], U8, "z_scales1")]
+        pairs = N_TILES // 2
+        sums = [[bank(pairs * half + pair) for pair in range(pairs)] for half in range(2)]
+
+        def quantize_z(b, ms):
+            nc.vector.quantize_mx(
+                out=z_codes[b][:, ms].bitcast(FP8X4),
+                scales=z_scales[b][:, ms],
+                in_=z_grouped[b][:, ms, :].rearrange("p m i -> p (m i)"),
+            )
+
+        def second_product(b, half):
+            for pair in range(pairs):
+                for place in range(BANK // P):
+                    n = 2 * pair + place * P // HALF
+                    first = half * HALF + place * P % HALF
+                    ms = slice(first, first + P)
+                    nc.tensor.matmul_mx(
+                        out=sums[half][pair][:, place * P : (place + 1) * P],
+                        lhsT=w2_sb[:, b, 2 * n * P : 2 * (n + 1) * P].bitcast(FP4X4),
+                        lhsT_scale=w2_sc[:, b, n * P : (n + 1) * P],
+                        rhs=z_codes[b][:, ms].bitcast(FP8X4),
+                        rhs_scale=z_scales[b][:, ms],
+                        start=(b == 0 and place == 0),
+                        stop=(b == H_PASSES - 1 and place == BANK // P - 1),
+                    )
+
+        quantize_z(0, WHOLE)
         for half in range(2):
-            second_product(0, half, z_scales[0])
-        x_last = stage(z_stage[0], [P, M], F32, "x_last")
-        total = keep.tile([P, M], F32, name="total")
-        logs = logs_tile(last)
-        for ms, ls in zip(halves, list_halves):
-            gather(last, x_last[:, ms], ms, ls)
-        for ms in halves:
-            nc.vector.tensor_tensor(total[:, ms], x_last[:, ms], rock_sb[1][:, PACK - 1, ms], ALU.add)
-            nc.scalar.activation(out=logs[:, ms], in_=total[:, ms], func=ACT.Ln)
-        for ms in halves:
-            nc.vector.tensor_scalar(z_grouped[1][:, ms, PACK - 1], logs[:, ms], gz_sb[1][:, PACK - 1 : PACK], None, ALU.mult)
+            second_product(0, half)
+
+        x_last = new_tile([P, M], F32, "x_last", z_grouped_tags[0])
+        total_last = new_tile([P, M], F32, "total_last")
+        logs_last = logs_tile(LAST)
+        for ms, ls in zip(HALVES, LIST_HALVES):
+            gather(LAST, x_last[:, ms], ms, ls)
+        for ms in HALVES:
+            nc.vector.tensor_tensor(total_last[:, ms], x_last[:, ms], exp_rock[1][:, PACK - 1, ms], ALU.add)
+            nc.scalar.activation(out=logs_last[:, ms], in_=total_last[:, ms], func=ACT.Ln)
+        for ms in HALVES:
+            gz_last = gz_sb[1][:, PACK - 1 :]
+            nc.vector.tensor_scalar(z_grouped[1][:, ms, PACK - 1], logs_last[:, ms], gz_last, None, ALU.mult)
         for half in range(2):
-            quantize_z(1, z_grouped[1], z_scales[1], halves[half])
-            second_product(1, half, z_scales[1])
+            quantize_z(1, HALVES[half])
+            second_product(1, half)
+
         for half in range(2):
-            for pair in range(N_TILES // 2):
-                result = keep.tile([P, 2, HALF], F32, name="result%d%d" % (half, pair))
+            for pair in range(pairs):
+                result = new_tile([P, 2, HALF], F32, "result%d%d" % (half, pair))
                 for j in range(2):
-                    n = 2 * pair + j
-                    sums = acc2[half][pair][:, j * HALF : (j + 1) * HALF]
-                    if (3 * half + pair) % 2 == 0:
-                        nc.scalar.activation(out=result[:, j, :], in_=sums, func=ACT.Identity, bias=b2_sb[:, n : n + 1])
+                    bias = b2_sb[:, 2 * pair + j : 2 * pair + j + 1]
+                    part = sums[half][pair][:, j * HALF : (j + 1) * HALF]
+                    if (pairs * half + pair) % 2 == 0:
+                        nc.scalar.activation(out=result[:, j, :], in_=part, func=ACT.Identity, bias=bias)
                     else:
-                        nc.vector.tensor_scalar(result[:, j, :], sums, b2_sb[:, n : n + 1], None, ALU.add)
-                rows = out[2 * pair * P : 2 * (pair + 1) * P, halves[half]]
+                        nc.vector.tensor_scalar(result[:, j, :], part, bias, None, ALU.add)
+                rows = out[2 * pair * P : 2 * (pair + 1) * P, HALVES[half]]
                 nc.sync.dma_start(out=rows.rearrange("(j p) m -> p j m", p=P), in_=result[:])

@@ -34,7 +34,7 @@ HALVES = [slice(0, HALF), slice(HALF, 2 * HALF)]
 LIST_HALVES = [slice(0, HALF // 16), slice(HALF // 16, 2 * HALF // 16)]
 WHOLE = slice(0, 2 * HALF)
 WHOLE_LIST = slice(0, 2 * HALF // 16)
-PAGES = PACK
+PAGES = 3
 SUM_BANK, BACK_BANK = 7, 6
 
 

from contextlib import ExitStack

import concourse.mybir as mybir
from concourse.masks import make_identity

T, S, M, T2, K, H, N = 2048, 512, 512, 1024, 1536, 1024, 768
FLOPS = 2 * K * H * S + 2 * H * N * M

F32 = mybir.dt.float32
BF16 = mybir.dt.bfloat16
I32 = mybir.dt.int32
U32 = mybir.dt.uint32
U16 = mybir.dt.uint16
U8 = mybir.dt.uint8
FP8X4 = mybir.dt.float8_e4m3fn_x4
FP4X4 = mybir.dt.float4_e2m1fn_x4
ACT = mybir.ActivationFunctionType
ALU = mybir.AluOpType

P = 128
PACK = 4
KP = P * PACK
K_PASSES = K // KP
H_PASSES = H // KP
ROW_TILES = H_PASSES * PACK
LAST = ROW_TILES - 1
N_TILES = N // P
M_TILES = M // P
QUADRANTS = 4
SCALE_ROWS = 4
BANK = 512
HALF = 256
HALVES = [slice(0, HALF), slice(HALF, 2 * HALF)]
LIST_HALVES = [slice(0, HALF // 16), slice(HALF // 16, 2 * HALF // 16)]
WHOLE = slice(0, 2 * HALF)
WHOLE_LIST = slice(0, 2 * HALF // 16)
PAGES = 3
SUM_BANK, BACK_BANK = 7, 6


def tile_list_pyramid_void_scores_kernel(
    tc, tab_words, tab_scales, offs, w1, gain, offs2, wgs, offs3, wgt, rock, gz, w2_words, w2_scales, b2, out
):
    nc = tc.nc
    with ExitStack() as ctx:
        keep = ctx.enter_context(tc.tile_pool(name="keep", bufs=1))
        psum = ctx.enter_context(tc.psum_pool(name="psum", bufs=1))

        def bank(number):
            return psum.tile([P, BANK], F32, name="bank%d" % number, tag="bank%d" % number)

        def new_tile(shape, dtype, name, tag=None):
            return keep.tile(shape, dtype, name=name, tag=tag or name, align_bytes=64)

        list1 = new_tile([P, S // 16], U16, "list1")
        list2 = new_tile([P, S // 16], U16, "list2")
        list3 = new_tile([P, M // 16], U16, "list3")
        w1_raw = [[new_tile([P, PACK, KP], F32, "w1_raw%d%d" % (b, a)) for a in range(K_PASSES)] for b in range(H_PASSES)]
        w1_scales = [[new_tile([P, KP], U8, "w1_scales%d%d" % (b, a)) for a in range(K_PASSES)] for b in range(H_PASSES)]
        w1_codes = {}
        tab_sb = [new_tile([P, T], I32, "tab%d" % a) for a in range(K_PASSES)]
        tab_sc = new_tile([P, T], U8, "tab_sc")
        v_codes = [new_tile([P, S], U32, "v_codes%d" % a) for a in range(K_PASSES)]
        v_scales = new_tile([P, S], U8, "v_scales")
        gain_sb = new_tile([P, H_PASSES, PACK], F32, "gain_sb")
        ln_gain = [new_tile([P, PACK], F32, "ln_gain%d" % b) for b in range(H_PASSES)]
        gz_sb = [new_tile([P, PACK], F32, "gz%d" % b) for b in range(H_PASSES)]
        b2_sb = new_tile([P, N_TILES], F32, "b2_sb")
        wgs_sb = new_tile([P, S], F32, "wgs_sb")
        wgt_sb = new_tile([P, M], F32, "wgt_sb")
        exp_rock = [new_tile([P, PACK, M], F32, "exp_rock%d" % b) for b in range(H_PASSES)]
        w2_sb = new_tile([P, H_PASSES, 2 * N], U8, "w2_sb")
        w2_sc = new_tile([P, H_PASSES, N], U8, "w2_sc")
        pages = [new_tile([P, T2], F32, "page%d" % number) for number in range(PAGES)]
        h = [new_tile([P, S], F32, "h%d" % t) for t in range(ROW_TILES)]
        z_codes = [new_tile([P, M], U32, "z_codes%d" % b) for b in range(H_PASSES)]
        ident = new_tile([P, P], F32, "ident")

        nc.vector.memset(tab_sc[:].bitcast(I32), 0)
        nc.vector.memset(w2_sc[:].rearrange("p b n -> p (b n)").bitcast(I32), 0)
        for page in pages:
            nc.vector.memset(page[:], 0.0)
        make_identity(nc, ident[:])

        def load_w1(b, a):
            rows = w1[a * KP : (a + 1) * KP, b * KP : (b + 1) * KP]
            nc.sync.dma_start(out=w1_raw[b][a][:], in_=rows.rearrange("(p j) r -> p j r", j=PACK))

        gz_rows = gz.rearrange("(b p i) -> p b i", p=P, i=PACK)
        nc.sync.dma_start(list1[:], offs)
        load_w1(0, 0)
        nc.sync.dma_start(out=gain_sb[:], in_=gain.rearrange("(b p i) -> p b i", p=P, i=PACK))
        nc.sync.dma_start(list2[:], offs2)
        nc.sync.dma_start(out=gz_sb[0][:], in_=gz_rows[:, 0, :])
        nc.sync.dma_start(list3[:], offs3)
        load_w1(0, 1)
        load_w1(0, 2)
        nc.sync.dma_start(out=gz_sb[1][:], in_=gz_rows[:, 1, :])
        for q in range(QUADRANTS):
            nc.sync.dma_start(
                out=tab_sc[32 * q : 32 * q + SCALE_ROWS * K_PASSES, :].bitcast(I32),
                in_=tab_scales[:, SCALE_ROWS * q : SCALE_ROWS * (q + 1), :].bitcast(I32),
            )
        for a in range(K_PASSES):
            nc.sync.dma_start(out=tab_sb[a][:], in_=tab_words[a].rearrange("p t i -> p (t i)").bitcast(I32))
        nc.sync.dma_start(out=wgs_sb[:], in_=wgs)
        for a in range(K_PASSES):
            load_w1(1, a)
        nc.sync.dma_start(out=wgt_sb[:], in_=wgt)
        for b in reversed(range(H_PASSES)):
            rows = rock[b * KP : (b + 1) * KP, :]
            nc.sync.dma_start(out=exp_rock[b][:], in_=rows.rearrange("(p i) m -> p i m", i=PACK))
        nc.sync.dma_start(out=w2_sb[:].bitcast(I32), in_=w2_words.rearrange("b p c -> p b c").bitcast(I32))
        for q in range(QUADRANTS):
            nc.sync.dma_start(
                out=w2_sc[32 * q : 32 * q + SCALE_ROWS, :, :].bitcast(I32),
                in_=w2_scales[:, SCALE_ROWS * q : SCALE_ROWS * (q + 1), :].rearrange("b s n -> s b n").bitcast(I32),
            )
        with nc.allow_non_contiguous_dma(reason="one bias value for each partition"):
            nc.sync.dma_start(out=b2_sb[:], in_=b2.rearrange("(n p) -> p n", p=P))

        for b in range(H_PASSES):
            nc.scalar.activation(out=ln_gain[b][:], in_=gain_sb[:, b, :], func=ACT.Ln)
        warm_up = new_tile([P, 1], F32, "warm_up")
        nc.scalar.activation(out=warm_up[:], in_=ln_gain[1][:, 0:1], func=ACT.Exp)

        def quantize_w1(b, a, copy=nc.scalar.copy, grouped_tag=None, codes_tag=None):
            grouped = new_tile([P, PACK, P, PACK], BF16, "w1_grouped%d%d" % (b, a), grouped_tag or "stage%d" % a)
            copy(
                out=grouped[:].rearrange("p i c j -> p c i j"),
                in_=w1_raw[b][a][:].rearrange("p j (c i) -> p c i j", i=PACK),
            )
            w1_codes[b, a] = new_tile([P, KP], U32, "w1_codes%d%d" % (b, a), codes_tag)
            nc.vector.quantize_mx(
                out=w1_codes[b, a][:].bitcast(FP8X4),
                scales=w1_scales[b][a][:],
                in_=grouped[:].rearrange("p i c j -> p (i c j)"),
            )

        def gather_words(a, js=WHOLE, ls=WHOLE_LIST):
            nc.vector.tensor_copy(v_codes[a][:, js], tab_sb[a][:].bitcast(U32).indirect(list1[:, ls]))

        def first_product(b, work):
            for a, i, js, acc in work:
                cols = slice(i * P, (i + 1) * P)
                nc.tensor.matmul_mx(
                    out=acc[:, js],
                    lhsT=w1_codes[b, a][:, cols].bitcast(FP8X4),
                    lhsT_scale=w1_scales[b][a][:, cols],
                    rhs=v_codes[a][:, js].bitcast(FP8X4),
                    rhs_scale=v_scales[SCALE_ROWS * a :, js],
                    start=(a == 0),
                    stop=(a == K_PASSES - 1),
                )
            for a, i, js, acc in work:
                if a == K_PASSES - 1:
                    bias = ln_gain[b][:, i : i + 1]
                    nc.scalar.activation(out=h[PACK * b + i][:, js], in_=acc[:, js], func=ACT.Exp, bias=bias)

        nc.vector.tensor_copy(v_scales[:], tab_sc[:].indirect(list1[:]))
        quantize_w1(0, 0, copy=nc.vector.tensor_copy)
        quantize_w1(0, 1)
        gather_words(0)
        quantize_w1(0, 2, codes_tag="tab0")
        gather_words(1)
        for js, ls in zip(HALVES, LIST_HALVES):
            gather_words(2, js, ls)
        banks = [bank(i) for i in range(PACK)]
        pieces = [(0, HALVES[0], banks[0]), (0, HALVES[1], bank(PACK))] + [(i, WHOLE, banks[i]) for i in range(1, PACK)]
        first_product(0, [(a, i, js, acc) for i, js, acc in pieces for a in range(K_PASSES)])
        quantize_w1(1, 0, grouped_tag="ln_gain0")
        quantize_w1(1, 1)
        quantize_w1(1, 2)
        banks = [bank(PACK + i) for i in range(PACK)]
        first_product(1, [(a, i, WHOLE, banks[i]) for a in range(K_PASSES) for i in range(PACK)])
        for b in reversed(range(H_PASSES)):
            nc.scalar.activation(out=exp_rock[b][:], in_=exp_rock[b][:], func=ACT.Exp)

        page_of = [pages[t % PAGES] for t in range(LAST)] + [pages[(LAST - 2) % PAGES]]

        def scatter(t, js=WHOLE, ls=WHOLE_LIST):
            nc.vector.tensor_tensor(page_of[t][:].indirect(list2[:, ls]), h[t][:, js], wgs_sb[:, js], ALU.mult)

        def gather(t, x, ms=WHOLE, ls=WHOLE_LIST):
            nc.vector.tensor_tensor(x, page_of[t][:].indirect(list3[:, ls]), wgt_sb[:, ms], ALU.mult)

        def logs_tile(t):
            number = t % 2 if t <= PACK else (t - PACK) // 2
            return new_tile([P, M], F32, "logs%d" % t, "logs%d" % number)

        def log_and_scale(t, x, grouped):
            b, i = divmod(t, PACK)
            total = bank(SUM_BANK - 2 * (t % 2))
            blocks = [(term, c) for term in (exp_rock[b][:, i, :], x) for c in range(M_TILES)]
            for number, (term, c) in enumerate(blocks):
                cols = slice(c * P, (c + 1) * P)
                nc.tensor.matmul(
                    total[:, cols],
                    term[:, cols],
                    ident[:],
                    is_transpose=True,
                    start=(number == 0),
                    stop=(number == len(blocks) - 1),
                )
            logs = logs_tile(t)
            nc.scalar.activation(out=logs[:], in_=total[:], func=ACT.Ln)
            back = bank(BACK_BANK - 2 * (t % 2))
            for c in range(M_TILES):
                cols = slice(c * P, (c + 1) * P)
                nc.tensor.transpose(back[:, cols], logs[:, cols], ident[:])
            nc.scalar.activation(out=grouped[:, :, i], in_=back[:], func=ACT.Copy, scale=gz_sb[b][:, i : i + 1])

        x_pair_tags = ["stage2", "stage1", "stage0", "x6"]
        z_grouped_tags = ["z_grouped0", "stage1"]
        z_grouped = []
        for js, ls in zip(HALVES, LIST_HALVES):
            scatter(0, js, ls)
        for t in range(LAST):
            b, i = divmod(t, PACK)
            if t + 1 < LAST:
                scatter(t + 1)
            if t % 2 == 0:
                x_pair = new_tile([P, 2, M], F32, "x_pair%d" % t, x_pair_tags[t // 2])
            x = new_tile([P, M], F32, "x5", "h%d" % (t + 1))[:] if t == LAST - 2 else x_pair[:, t % 2, :]
            gather(t, x)
            if i == 0:
                z_grouped.append(new_tile([P, M, PACK], BF16, "z_grouped%d" % b, z_grouped_tags[b]))
            log_and_scale(t, x, z_grouped[b])
        scatter(LAST)

        z_scales = [new_tile([P, M], U8, "z_scales0", "ident"), new_tile([P, M], U8, "z_scales1")]
        pairs = N_TILES // 2
        sums = [[bank(pairs * half + pair) for pair in range(pairs)] for half in range(2)]

        def quantize_z(b, ms):
            nc.vector.quantize_mx(
                out=z_codes[b][:, ms].bitcast(FP8X4),
                scales=z_scales[b][:, ms],
                in_=z_grouped[b][:, ms, :].rearrange("p m i -> p (m i)"),
            )

        def second_product(b, half):
            for pair in range(pairs):
                for place in range(BANK // P):
                    n = 2 * pair + place * P // HALF
                    first = half * HALF + place * P % HALF
                    ms = slice(first, first + P)
                    nc.tensor.matmul_mx(
                        out=sums[half][pair][:, place * P : (place + 1) * P],
                        lhsT=w2_sb[:, b, 2 * n * P : 2 * (n + 1) * P].bitcast(FP4X4),
                        lhsT_scale=w2_sc[:, b, n * P : (n + 1) * P],
                        rhs=z_codes[b][:, ms].bitcast(FP8X4),
                        rhs_scale=z_scales[b][:, ms],
                        start=(b == 0 and place == 0),
                        stop=(b == H_PASSES - 1 and place == BANK // P - 1),
                    )

        quantize_z(0, WHOLE)
        for half in range(2):
            second_product(0, half)

        x_last = new_tile([P, M], F32, "x_last", z_grouped_tags[0])
        total_last = new_tile([P, M], F32, "total_last")
        logs_last = logs_tile(LAST)
        for ms, ls in zip(HALVES, LIST_HALVES):
            gather(LAST, x_last[:, ms], ms, ls)
        for ms in HALVES:
            nc.vector.tensor_tensor(total_last[:, ms], x_last[:, ms], exp_rock[1][:, PACK - 1, ms], ALU.add)
            nc.scalar.activation(out=logs_last[:, ms], in_=total_last[:, ms], func=ACT.Ln)
        for ms in HALVES:
            gz_last = gz_sb[1][:, PACK - 1 :]
            nc.vector.tensor_scalar(z_grouped[1][:, ms, PACK - 1], logs_last[:, ms], gz_last, None, ALU.mult)
        for half in range(2):
            quantize_z(1, HALVES[half])
            second_product(1, half)

        for half in range(2):
            for pair in range(pairs):
                result = new_tile([P, 2, HALF], F32, "result%d%d" % (half, pair))
                for j in range(2):
                    bias = b2_sb[:, 2 * pair + j : 2 * pair + j + 1]
                    part = sums[half][pair][:, j * HALF : (j + 1) * HALF]
                    if (pairs * half + pair) % 2 == 0:
                        nc.scalar.activation(out=result[:, j, :], in_=part, func=ACT.Identity, bias=bias)
                    else:
                        nc.vector.tensor_scalar(result[:, j, :], part, bias, None, ALU.add)
                rows = out[2 * pair * P : 2 * (pair + 1) * P, HALVES[half]]
                nc.sync.dma_start(out=rows.rearrange("(j p) m -> p j m", p=P), in_=result[:])
